import numpy as np, ml_dtypes
CORES = [30,158,46,174,86,214]
N = 6
S, B = 3, 128
def setup_inputs(rng):
    a = (rng.standard_normal((128, 128), dtype=np.float32) / 12).astype(ml_dtypes.bfloat16)
    return {"x": rng.standard_normal((N, 128, S * B), dtype=np.float32).astype(ml_dtypes.bfloat16), "a": np.broadcast_to(a, (N, 128, 128)).copy(), "at": np.broadcast_to(a.T, (N, 128, 128)).copy()}
def setup_inputs_big(rng):
    d = setup_inputs(rng)
    for k in ("x",): d[k] = (d[k].astype(np.float32) * 1048576.0).astype(d[k].dtype)
    return d
def setup_inputs_small(rng):
    d = setup_inputs(rng)
    for k in ("x",): d[k] = (d[k].astype(np.float32) * (1 / 1048576.0)).astype(d[k].dtype)
    return d
def setup_inputs_apart(rng):
    d = setup_inputs(rng)
    f = (10.0 ** rng.permutation(np.linspace(-1.5, 1.5, N))).astype(np.float32).reshape(N, 1, 1)
    for k in ("x",): d[k] = (d[k].astype(np.float32) * f).astype(d[k].dtype)
    return d
def reference(x, a, at):
    X, A = x.astype(np.float64), a.astype(np.float64)
    y = np.zeros((N, 128, S * B)); h = np.zeros((128, B))
    for r in range(N):
        for s in range(S):
            h = A[r].T @ h + X[r][:, B * s:B * s + B]
            y[r][:, B * s:B * s + B] = h
    return {"y": y.astype(ml_dtypes.bfloat16)}

@@ -1,0 +1,150 @@
+from concourse.bass import DstId, RemoteDMATransfer
+from concourse.mybir import AluOpType
+
+B = 128
+S = 3
+NR = 6
+NPOOL = 40
+
+SCRATCH = {
+    "xs": ("sbuf", [128, S * B], "bfloat16"),
+    "pw": ("sbuf", [128, 16 * B], "bfloat16"),
+    "tp": ("sbuf", [128, 4 * B], "bfloat16"),
+    "hl": ("sbuf", [128, 2 * B], "bfloat16"),
+    "land": ("sbuf", [128, (NR - 1) * B], "bfloat16"),
+    "yo": ("sbuf", [128, S * B], "bfloat16"),
+    "py0": ("psum", [128, 512], "float32"),
+    "py1": ("psum", [128, 512], "float32"),
+    "py2": ("psum", [128, 512], "float32"),
+    "pl": ("psum", [128, 512], "float32"),
+    "pp0": ("psum", [128, 512], "float32"),
+    "pp1": ("psum", [128, 512], "float32"),
+    "pp2": ("psum", [128, 512], "float32"),
+    "pp3": ("psum", [128, 512], "float32"),
+}
+SEMAPHORES = ["arr%d" % j for j in range(NR - 1)] + ["sent"] + ["q%d" % i for i in range(NPOOL)]
+
+
+def _blk(buf, i, k=1):
+    return buf[:, i * B:(i + k) * B]
+
+
+def _send_mask(topo, cores, j):
+    m = None
+    for d in cores[j + 1:]:
+        assert topo.may_write(cores[j], d)
+        m = topo.mask(cores[j], d) if m is None else (m & topo.mask(cores[j], d))
+    return m
+
+
+def rank_program(g, core, T, topo):
+    r = T.rank_of(core)
+    if r is None:
+        return
+    cores = list(T.cores)
+    queues = {"t": g.tensor, "v": g.vector, "g": g, "sy": g.sync, "sc": g.scalar}
+    seen = {"t": set(), "v": set(), "g": set(), "sy": set(), "sc": set()}
+    cnt = [0]
+
+    def done(instrs, amount):
+        k = cnt[0]
+        cnt[0] += 1
+        for ins in instrs:
+            ins.then_inc(T.sem["q%d" % k], amount)
+        return (k, amount * len(instrs))
+
+    def need(q, *tokens):
+        for k, val in tokens:
+            if k not in seen[q]:
+                seen[q].add(k)
+                queues[q].wait_ge(T.sem["q%d" % k], val)
+
+    def mm(out, lhsT, rhs, start=True, stop=True):
+        return g.tensor.matmul(out=out, lhsT=lhsT, rhs=rhs, start=start, stop=stop)
+
+    tx = done([g.sync.dma_start(T.xs[:], T.x[:])], 16)
+    tokA = {1: done([g.scalar.dma_start(_blk(T.pw, 0), T.a[:])], 16)}
+    tokT = {}
+    if r > 0:
+        tokT[1] = done([g.scalar.dma_start(_blk(T.tp, 0), T.at[:])], 16)
+
+    need("t", tx, tokA[1])
+    m1 = done([mm(T.pl[:, 0:B], _blk(T.pw, 0), _blk(T.xs, 0))], 1)
+    need("v", tx, m1)
+    t1 = done([g.vector.tensor_tensor(out=_blk(T.hl, 0), in0=T.pl[:, 0:B], in1=_blk(T.xs, 1), op=AluOpType.add)], 1)
+    need("t", t1)
+    m2 = done([mm(T.pl[:, B:2 * B], _blk(T.pw, 0), _blk(T.hl, 0))], 1)
+    need("v", m2)
+    t2 = done([g.vector.tensor_tensor(out=_blk(T.hl, 1), in0=T.pl[:, B:2 * B], in1=_blk(T.xs, 2), op=AluOpType.add)], 1)
+
+    later = cores[r + 1:]
+    if later:
+        mask = _send_mask(topo, cores, r)
+        ids = []
+        for d in later:
+            rid, pid = topo.addr(d, core)
+            ids.append(DstId(rid=rid, pnc=pid))
+        need("g", t2)
+        g.remote_dma_fused([RemoteDMATransfer(dst_ids=ids, dma_engine_mask=mask, remote_sem=T.sem["arr%d" % r],
+                                              srcs=[_blk(T.hl, 1)], dsts=[_blk(T.land, r) for d in later],
+                                              alu_op=0)], local_sem=T.sem.sent)
+        g.wait_ge(T.sem.sent, bin(mask).count("1"))
+
+    if r == 0:
+        need("sc", tx)
+        st0 = done([g.scalar.dma_start(T.y[:, 0:B], _blk(T.xs, 0))], 16)
+        need("sy", t1, t2)
+        st1 = done([g.sync.dma_start(T.y[:, B:S * B], T.hl[:])], 16)
+        need("sc", st0)
+        need("sy", st1)
+        return
+
+    npow = S * r
+    banks = [T.pp0, T.pp1, T.pp2, T.pp3]
+    nb = [0]
+
+    def bank():
+        b = banks[nb[0] % len(banks)]
+        nb[0] += 1
+        return b
+
+    k, lev = 1, 0
+    while k < npow:
+        if 2 * k < npow:
+            need("t", tokA[k], tokT[k])
+            pb = bank()
+            m = done([mm(pb[:, 0:B], _blk(T.pw, k - 1), _blk(T.tp, lev))], 1)
+            need("v", m)
+            tokT[2 * k] = done([g.vector.tensor_copy(out=_blk(T.tp, lev + 1), in_=pb[:, 0:B])], 1)
+        hi = min(2 * k, npow)
+        for lo in range(k + 1, hi + 1, 4):
+            w = min(4, hi - lo + 1)
+            need("t", tokT[k], *[tokA[p - k] for p in range(lo, lo + w)])
+            pb = bank()
+            m = done([mm(pb[:, 0:w * B], _blk(T.tp, lev), _blk(T.pw, lo - k - 1, w))], 1)
+            need("v", m)
+            tok = done([g.vector.tensor_copy(out=_blk(T.pw, lo - 1, w), in_=pb[:, 0:w * B])], 1)
+            for p in range(lo, lo + w):
+                tokA[p] = tok
+        k, lev = 2 * k, lev + 1
+
+    need("t", *[tokA[p] for p in range(1, npow + 1)])
+    py = [T.py0, T.py1, T.py2]
+    my = [None] * S
+    for j in range(r - 1, -1, -1):
+        g.tensor.wait_ge(T.sem["arr%d" % j], bin(_send_mask(topo, cores, j)).count("1"))
+        for s in range(S):
+            ins = mm(py[s][:, 0:B], _blk(T.pw, S * (r - 1 - j) + s), _blk(T.land, j), start=(j == r - 1), stop=(j == 0))
+            if j == 0:
+                my[s] = done([ins], 1)
+
+    need("v", t1, t2)
+    loc = [_blk(T.xs, 0), _blk(T.hl, 0), _blk(T.hl, 1)]
+    fin = []
+    for s in range(S):
+        need("v", my[s])
+        fin.append(g.vector.tensor_tensor(out=_blk(T.yo, s), in0=py[s][:, 0:B], in1=loc[s], op=AluOpType.add))
+    ty = done(fin, 1)
+    need("sy", ty)
+    st = done([g.sync.dma_start(T.y[:], T.yo[:])], 16)
+    need("sy", st)

@@ -2,16 +2,18 @@ from concourse.bass import DstId, RemoteDMATransfer
 from concourse.mybir import AluOpType
 
 B = 128
+H = B // 2
 S = 3
 NR = 6
-NPOOL = 40
+NPOOL = 44
 
 SCRATCH = {
     "xs": ("sbuf", [128, S * B], "bfloat16"),
+    "lx": ("sbuf", [128, S * B], "bfloat16"),
     "pw": ("sbuf", [128, 16 * B], "bfloat16"),
     "tp": ("sbuf", [128, 4 * B], "bfloat16"),
     "hl": ("sbuf", [128, 2 * B], "bfloat16"),
-    "land": ("sbuf", [128, (NR - 1) * B], "bfloat16"),
+    "land": ("sbuf", [128, (NR - 2) * B], "bfloat16"),
     "yo": ("sbuf", [128, S * B], "bfloat16"),
     "py0": ("psum", [128, 512], "float32"),
     "py1": ("psum", [128, 512], "float32"),
@@ -22,7 +24,7 @@ SCRATCH = {
     "pp2": ("psum", [128, 512], "float32"),
     "pp3": ("psum", [128, 512], "float32"),
 }
-SEMAPHORES = ["arr%d" % j for j in range(NR - 1)] + ["sent"] + ["q%d" % i for i in range(NPOOL)]
+SEMAPHORES = ["arr%d" % j for j in range(NR - 2)] + ["arx", "sent"] + ["q%d" % i for i in range(NPOOL)]
 
 
 def _blk(buf, i, k=1):
@@ -42,6 +44,9 @@ def rank_program(g, core, T, topo):
     if r is None:
         return
     cores = list(T.cores)
+    n = len(cores)
+    last = r == n - 1
+    carries = r + 2 < n
     queues = {"t": g.tensor, "v": g.vector, "g": g, "sy": g.sync, "sc": g.scalar}
     seen = {"t": set(), "v": set(), "g": set(), "sy": set(), "sc": set()}
     cnt = [0]
@@ -62,44 +67,73 @@ def rank_program(g, core, T, topo):
     def mm(out, lhsT, rhs, start=True, stop=True):
         return g.tensor.matmul(out=out, lhsT=lhsT, rhs=rhs, start=start, stop=stop)
 
+    def add(out, in0, in1):
+        return g.vector.tensor_tensor(out=out, in0=in0, in1=in1, op=AluOpType.add)
+
+    def engines(j):
+        return bin(_send_mask(topo, cores, j)).count("1")
+
+    tokA, tokT = {}, {}
+    tokA[1] = done([g.scalar.dma_start(_blk(T.pw, 0), T.a[:])], 16)
+    if last:
+        tokT[1] = done([g.sync.dma_start(_blk(T.tp, 0), T.at[:])], 16)
     tx = done([g.sync.dma_start(T.xs[:], T.x[:])], 16)
-    tokA = {1: done([g.scalar.dma_start(_blk(T.pw, 0), T.a[:])], 16)}
-    tokT = {}
-    if r > 0:
+    if 0 < r and not last:
         tokT[1] = done([g.scalar.dma_start(_blk(T.tp, 0), T.at[:])], 16)
 
-    need("t", tx, tokA[1])
-    m1 = done([mm(T.pl[:, 0:B], _blk(T.pw, 0), _blk(T.xs, 0))], 1)
-    need("v", tx, m1)
-    t1 = done([g.vector.tensor_tensor(out=_blk(T.hl, 0), in0=T.pl[:, 0:B], in1=_blk(T.xs, 1), op=AluOpType.add)], 1)
-    need("t", t1)
-    m2 = done([mm(T.pl[:, B:2 * B], _blk(T.pw, 0), _blk(T.hl, 0))], 1)
-    need("v", m2)
-    t2 = done([g.vector.tensor_tensor(out=_blk(T.hl, 1), in0=T.pl[:, B:2 * B], in1=_blk(T.xs, 2), op=AluOpType.add)], 1)
+    sent = 0
+    if not last:
+        rid, pid = topo.addr(cores[r + 1], core)
+        need("g", tx)
+        g.remote_dma(out_ap=T.lx[:], in_ap=T.xs[:], remote_sem=T.sem.arx, local_sem=T.sem.sent, pid=pid,
+                     routing_id=rid, dma_engine_mask=_send_mask(topo, cores, r))
+        sent += engines(r)
 
-    later = cores[r + 1:]
-    if later:
-        mask = _send_mask(topo, cores, r)
+    tl = []
+    if carries:
+        a1 = _blk(T.pw, 0)
+        pb1, pb2 = [T.pl, T.py0], [T.py1, T.py2]
+        need("t", tx, tokA[1])
+        m1 = [done([mm(pb1[h][:, 0:H], a1, T.xs[:, h * H:(h + 1) * H])], 1) for h in range(2)]
+        need("v", tx)
+        t1 = []
+        for h in range(2):
+            need("v", m1[h])
+            t1.append(done([add(T.hl[:, h * H:(h + 1) * H], pb1[h][:, 0:H], T.xs[:, B + h * H:B + (h + 1) * H])], 1))
+        m2 = []
+        for h in range(2):
+            need("t", t1[h])
+            m2.append(done([mm(pb2[h][:, 0:H], a1, T.hl[:, h * H:(h + 1) * H])], 1))
+        fin2 = []
+        for h in range(2):
+            need("v", m2[h])
+            fin2.append(add(T.hl[:, B + h * H:B + (h + 1) * H], pb2[h][:, 0:H], T.xs[:, 2 * B + h * H:2 * B + (h + 1) * H]))
+        t2 = done(fin2, 1)
+        tl = t1 + [t2]
+
+        later = cores[r + 2:]
         ids = []
         for d in later:
             rid, pid = topo.addr(d, core)
             ids.append(DstId(rid=rid, pnc=pid))
         need("g", t2)
-        g.remote_dma_fused([RemoteDMATransfer(dst_ids=ids, dma_engine_mask=mask, remote_sem=T.sem["arr%d" % r],
-                                              srcs=[_blk(T.hl, 1)], dsts=[_blk(T.land, r) for d in later],
-                                              alu_op=0)], local_sem=T.sem.sent)
-        g.wait_ge(T.sem.sent, bin(mask).count("1"))
+        g.remote_dma_fused([RemoteDMATransfer(dst_ids=ids, dma_engine_mask=_send_mask(topo, cores, r),
+                                              remote_sem=T.sem["arr%d" % r], srcs=[_blk(T.hl, 1)],
+                                              dsts=[_blk(T.land, r) for d in later], alu_op=0)], local_sem=T.sem.sent)
+        sent += engines(r)
+    if sent:
+        g.wait_ge(T.sem.sent, sent)
 
     if r == 0:
         need("sc", tx)
         st0 = done([g.scalar.dma_start(T.y[:, 0:B], _blk(T.xs, 0))], 16)
-        need("sy", t1, t2)
+        need("sy", *tl)
         st1 = done([g.sync.dma_start(T.y[:, B:S * B], T.hl[:])], 16)
         need("sc", st0)
         need("sy", st1)
         return
 
-    npow = S * r
+    npow = max(S * r, 2 * S - 1)
     banks = [T.pp0, T.pp1, T.pp2, T.pp3]
     nb = [0]
 
@@ -128,22 +162,36 @@ def rank_program(g, core, T, topo):
                 tokA[p] = tok
         k, lev = 2 * k, lev + 1
 
-    need("t", *[tokA[p] for p in range(1, npow + 1)])
+    ops = []
+    if not carries:
+        ops += [(1, 1, _blk(T.xs, 0), None), (2, 2, _blk(T.xs, 0), None), (2, 1, _blk(T.xs, 1), None)]
+    for i in range(S - 1, -1, -1):
+        ops += [(s, s + S - i, _blk(T.lx, i), ("arx", r - 1)) for s in range(S)]
+    for j in range(r - 2, -1, -1):
+        ops += [(s, S * (r - 1 - j) + s + 1, _blk(T.land, j), ("arr%d" % j, j)) for s in range(S)]
+    first, final = {}, {}
+    for i, op in enumerate(ops):
+        first.setdefault(op[0], i)
+        final[op[0]] = i
+    need("t", tx, *tl)
     py = [T.py0, T.py1, T.py2]
     my = [None] * S
-    for j in range(r - 1, -1, -1):
-        g.tensor.wait_ge(T.sem["arr%d" % j], bin(_send_mask(topo, cores, j)).count("1"))
-        for s in range(S):
-            ins = mm(py[s][:, 0:B], _blk(T.pw, S * (r - 1 - j) + s), _blk(T.land, j), start=(j == r - 1), stop=(j == 0))
-            if j == 0:
-                my[s] = done([ins], 1)
+    landed = set()
+    for i, (s, p, rhs, src) in enumerate(ops):
+        if src is not None and src[0] not in landed:
+            landed.add(src[0])
+            g.tensor.wait_ge(T.sem[src[0]], engines(src[1]))
+        need("t", tokA[p])
+        ins = mm(py[s][:, 0:B], _blk(T.pw, p - 1), rhs, start=(first[s] == i), stop=(final[s] == i))
+        if final[s] == i:
+            my[s] = done([ins], 1)
 
-    need("v", t1, t2)
-    loc = [_blk(T.xs, 0), _blk(T.hl, 0), _blk(T.hl, 1)]
+    need("v", tx, *tl)
+    loc = [_blk(T.xs, 0), _blk(T.hl, 0), _blk(T.hl, 1)] if carries else [_blk(T.xs, s) for s in range(S)]
     fin = []
     for s in range(S):
         need("v", my[s])
-        fin.append(g.vector.tensor_tensor(out=_blk(T.yo, s), in0=py[s][:, 0:B], in1=loc[s], op=AluOpType.add))
+        fin.append(add(_blk(T.yo, s), py[s][:, 0:B], loc[s]))
     ty = done(fin, 1)
     need("sy", ty)
     st = done([g.sync.dma_start(T.y[:], T.yo[:])], 16)

from concourse.bass import DstId, RemoteDMATransfer
from concourse.mybir import AluOpType

B = 128
H = B // 2
S = 3
NR = 6
NPOOL = 44

SCRATCH = {
    "xs": ("sbuf", [128, S * B], "bfloat16"),
    "lx": ("sbuf", [128, S * B], "bfloat16"),
    "pw": ("sbuf", [128, 16 * B], "bfloat16"),
    "tp": ("sbuf", [128, 4 * B], "bfloat16"),
    "hl": ("sbuf", [128, 2 * B], "bfloat16"),
    "land": ("sbuf", [128, (NR - 2) * B], "bfloat16"),
    "yo": ("sbuf", [128, S * B], "bfloat16"),
    "py0": ("psum", [128, 512], "float32"),
    "py1": ("psum", [128, 512], "float32"),
    "py2": ("psum", [128, 512], "float32"),
    "pl": ("psum", [128, 512], "float32"),
    "pp0": ("psum", [128, 512], "float32"),
    "pp1": ("psum", [128, 512], "float32"),
    "pp2": ("psum", [128, 512], "float32"),
    "pp3": ("psum", [128, 512], "float32"),
}
SEMAPHORES = ["arr%d" % j for j in range(NR - 2)] + ["arx", "sent"] + ["q%d" % i for i in range(NPOOL)]


def _blk(buf, i, k=1):
    return buf[:, i * B:(i + k) * B]


def _send_mask(topo, cores, j):
    m = None
    for d in cores[j + 1:]:
        assert topo.may_write(cores[j], d)
        m = topo.mask(cores[j], d) if m is None else (m & topo.mask(cores[j], d))
    return m


def rank_program(g, core, T, topo):
    r = T.rank_of(core)
    if r is None:
        return
    cores = list(T.cores)
    n = len(cores)
    last = r == n - 1
    carries = r + 2 < n
    queues = {"t": g.tensor, "v": g.vector, "g": g, "sy": g.sync, "sc": g.scalar}
    seen = {"t": set(), "v": set(), "g": set(), "sy": set(), "sc": set()}
    cnt = [0]

    def done(instrs, amount):
        k = cnt[0]
        cnt[0] += 1
        for ins in instrs:
            ins.then_inc(T.sem["q%d" % k], amount)
        return (k, amount * len(instrs))

    def need(q, *tokens):
        for k, val in tokens:
            if k not in seen[q]:
                seen[q].add(k)
                queues[q].wait_ge(T.sem["q%d" % k], val)

    def mm(out, lhsT, rhs, start=True, stop=True):
        return g.tensor.matmul(out=out, lhsT=lhsT, rhs=rhs, start=start, stop=stop)

    def add(out, in0, in1):
        return g.vector.tensor_tensor(out=out, in0=in0, in1=in1, op=AluOpType.add)

    def engines(j):
        return bin(_send_mask(topo, cores, j)).count("1")

    tokA, tokT = {}, {}
    tokA[1] = done([g.scalar.dma_start(_blk(T.pw, 0), T.a[:])], 16)
    if last:
        tokT[1] = done([g.sync.dma_start(_blk(T.tp, 0), T.at[:])], 16)
    tx = done([g.sync.dma_start(T.xs[:], T.x[:])], 16)
    if 0 < r and not last:
        tokT[1] = done([g.scalar.dma_start(_blk(T.tp, 0), T.at[:])], 16)

    sent = 0
    if not last:
        rid, pid = topo.addr(cores[r + 1], core)
        need("g", tx)
        g.remote_dma(out_ap=T.lx[:], in_ap=T.xs[:], remote_sem=T.sem.arx, local_sem=T.sem.sent, pid=pid,
                     routing_id=rid, dma_engine_mask=_send_mask(topo, cores, r))
        sent += engines(r)

    tl = []
    if carries:
        a1 = _blk(T.pw, 0)
        pb1, pb2 = [T.pl, T.py0], [T.py1, T.py2]
        need("t", tx, tokA[1])
        m1 = [done([mm(pb1[h][:, 0:H], a1, T.xs[:, h * H:(h + 1) * H])], 1) for h in range(2)]
        need("v", tx)
        t1 = []
        for h in range(2):
            need("v", m1[h])
            t1.append(done([add(T.hl[:, h * H:(h + 1) * H], pb1[h][:, 0:H], T.xs[:, B + h * H:B + (h + 1) * H])], 1))
        m2 = []
        for h in range(2):
            need("t", t1[h])
            m2.append(done([mm(pb2[h][:, 0:H], a1, T.hl[:, h * H:(h + 1) * H])], 1))
        fin2 = []
        for h in range(2):
            need("v", m2[h])
            fin2.append(add(T.hl[:, B + h * H:B + (h + 1) * H], pb2[h][:, 0:H], T.xs[:, 2 * B + h * H:2 * B + (h + 1) * H]))
        t2 = done(fin2, 1)
        tl = t1 + [t2]

        later = cores[r + 2:]
        ids = []
        for d in later:
            rid, pid = topo.addr(d, core)
            ids.append(DstId(rid=rid, pnc=pid))
        need("g", t2)
        g.remote_dma_fused([RemoteDMATransfer(dst_ids=ids, dma_engine_mask=_send_mask(topo, cores, r),
                                              remote_sem=T.sem["arr%d" % r], srcs=[_blk(T.hl, 1)],
                                              dsts=[_blk(T.land, r) for d in later], alu_op=0)], local_sem=T.sem.sent)
        sent += engines(r)
    if sent:
        g.wait_ge(T.sem.sent, sent)

    if r == 0:
        need("sc", tx)
        st0 = done([g.scalar.dma_start(T.y[:, 0:B], _blk(T.xs, 0))], 16)
        need("sy", *tl)
        st1 = done([g.sync.dma_start(T.y[:, B:S * B], T.hl[:])], 16)
        need("sc", st0)
        need("sy", st1)
        return

    npow = max(S * r, 2 * S - 1)
    banks = [T.pp0, T.pp1, T.pp2, T.pp3]
    nb = [0]

    def bank():
        b = banks[nb[0] % len(banks)]
        nb[0] += 1
        return b

    k, lev = 1, 0
    while k < npow:
        if 2 * k < npow:
            need("t", tokA[k], tokT[k])
            pb = bank()
            m = done([mm(pb[:, 0:B], _blk(T.pw, k - 1), _blk(T.tp, lev))], 1)
            need("v", m)
            tokT[2 * k] = done([g.vector.tensor_copy(out=_blk(T.tp, lev + 1), in_=pb[:, 0:B])], 1)
        hi = min(2 * k, npow)
        for lo in range(k + 1, hi + 1, 4):
            w = min(4, hi - lo + 1)
            need("t", tokT[k], *[tokA[p - k] for p in range(lo, lo + w)])
            pb = bank()
            m = done([mm(pb[:, 0:w * B], _blk(T.tp, lev), _blk(T.pw, lo - k - 1, w))], 1)
            need("v", m)
            tok = done([g.vector.tensor_copy(out=_blk(T.pw, lo - 1, w), in_=pb[:, 0:w * B])], 1)
            for p in range(lo, lo + w):
                tokA[p] = tok
        k, lev = 2 * k, lev + 1

    ops = []
    if not carries:
        ops += [(1, 1, _blk(T.xs, 0), None), (2, 2, _blk(T.xs, 0), None), (2, 1, _blk(T.xs, 1), None)]
    for i in range(S - 1, -1, -1):
        ops += [(s, s + S - i, _blk(T.lx, i), ("arx", r - 1)) for s in range(S)]
    for j in range(r - 2, -1, -1):
        ops += [(s, S * (r - 1 - j) + s + 1, _blk(T.land, j), ("arr%d" % j, j)) for s in range(S)]
    first, final = {}, {}
    for i, op in enumerate(ops):
        first.setdefault(op[0], i)
        final[op[0]] = i
    need("t", tx, *tl)
    py = [T.py0, T.py1, T.py2]
    my = [None] * S
    landed = set()
    for i, (s, p, rhs, src) in enumerate(ops):
        if src is not None and src[0] not in landed:
            landed.add(src[0])
            g.tensor.wait_ge(T.sem[src[0]], engines(src[1]))
        need("t", tokA[p])
        ins = mm(py[s][:, 0:B], _blk(T.pw, p - 1), rhs, start=(first[s] == i), stop=(final[s] == i))
        if final[s] == i:
            my[s] = done([ins], 1)

    need("v", tx, *tl)
    loc = [_blk(T.xs, 0), _blk(T.hl, 0), _blk(T.hl, 1)] if carries else [_blk(T.xs, s) for s in range(S)]
    fin = []
    for s in range(S):
        need("v", my[s])
        fin.append(add(_blk(T.yo, s), py[s][:, 0:B], loc[s]))
    ty = done(fin, 1)
    need("sy", ty)
    st = done([g.sync.dma_start(T.y[:], T.yo[:])], 16)
    need("sy", st)
